import numpy as np
import ml_dtypes


def mxq(x, axis, fmt="e4m3"):
    dtype, down = {"e4m3": (ml_dtypes.float8_e4m3fn, 7), "e5m2": (ml_dtypes.float8_e5m2, 14)}[fmt]
    v = np.moveaxis(np.asarray(x, np.float32).astype(ml_dtypes.bfloat16).astype(np.float64), axis, -1)
    blocks = v.reshape(v.shape[:-1] + (-1, 32))
    amax = np.abs(blocks).max(-1, keepdims=True)
    byte = np.maximum(np.where(amax > 0, np.frexp(amax)[1] - 1 + 127, 0) - down, 1)
    scale = np.exp2(byte - 127.0)
    codes = (blocks / scale).astype(np.float32).astype(dtype).astype(np.float64)
    return np.moveaxis((codes * scale).reshape(v.shape), -1, axis)


WIDE = False


def mx_kscale(k):
    if not WIDE:
        return np.ones(k)
    levels = np.array([30, -30])
    if k % 512:
        return np.exp2(np.random.permutation(np.resize(levels, k // 32))).repeat(32)
    a = np.empty((k // 512, 16))
    for p in range(k // 512):
        a[p, :8] = np.random.permutation(np.resize(levels, 8))
        for g in range(8):
            far = levels[np.abs(levels - a[p, g]) >= 10]
            a[p, g + 8] = far[np.random.randint(len(far))]
    return np.exp2(a.ravel()).repeat(32)


BF16 = ml_dtypes.bfloat16


def bf(x):
    return np.asarray(x, np.float32).astype(BF16)


def f64(x):
    return np.asarray(x).astype(np.float64)


E2M1 = np.array([0.0, 0.5, 1.0, 1.5, 2.0, 3.0, 4.0, 6.0, -0.0, -0.5, -1.0, -1.5, -2.0, -3.0, -4.0, -6.0])


def pack_weight(w, fmt):
    k, n = w.shape
    w = f64(bf(w)).reshape(k // 32, 32, n)
    amax = np.abs(w).max(1)
    if fmt == "e4m3":
        byte = np.frexp(amax)[1] - 1 + 127 - 7
    else:
        mant, ex = np.frexp(amax / 6.0)
        byte = np.where(mant > 0.5, ex, ex - 1) + 127
    byte = np.clip(np.where(amax > 0, byte, 1), 1, 254)
    scaled = (w * np.exp2(127.0 - byte)[:, None, :]).reshape(k, n).astype(np.float32)
    by_word = np.ascontiguousarray(scaled.reshape(k // 512, 128, 4, n).transpose(0, 1, 3, 2))
    if fmt == "e4m3":
        words = by_word.astype(ml_dtypes.float8_e4m3fn).view(np.uint8)
    else:
        c = by_word.astype(ml_dtypes.float4_e2m1fn).view(np.uint8) & 0xF
        words = c[..., 0::2] | (c[..., 1::2] << 4)
    return np.ascontiguousarray(words), np.ascontiguousarray(byte.astype(np.uint8).reshape(k // 512, 16, n))


def unpack_weight(words, scales, fmt):
    g, p, n, _ = words.shape
    if fmt == "e4m3":
        vals = np.ascontiguousarray(words).view(ml_dtypes.float8_e4m3fn).astype(np.float64)
    else:
        nib = np.empty((g, p, n, 4), np.uint8)
        nib[..., 0::2] = words & 0xF
        nib[..., 1::2] = words >> 4
        vals = E2M1[nib]
    vals = vals * np.repeat(np.exp2(scales.astype(np.float64) - 127.0), 8, axis=1)[..., None]
    return vals.transpose(0, 1, 3, 2).reshape(g * 512, n)
def pack4(w):
    words, scales = pack_weight(w, "e2m1")
    return words.reshape(words.shape[0], 128, -1), scales


def unpack4(words, scales):
    return unpack_weight(words.reshape(words.shape[0], 128, -1, 2), scales, "e2m1")


S, K, C, F = 2048, 1536, 1024, 512


def setup_inputs():
    s, u = mx_kscale(K), mx_kscale(S)
    head = np.random.standard_normal((K, C)) / np.sqrt(K) / s[:, None]
    head_words, head_scales = pack4(head)
    return {"hidden": bf(np.random.standard_normal((S, K)) * s),
            "head_words": head_words,
            "head_scales": head_scales,
            "base": bf(0.5 * np.random.standard_normal(C)),
            "omega": bf(np.exp(0.5 * np.random.standard_normal(S)) * u),
            "pinv": bf(np.random.standard_normal((F, S)) / np.sqrt(S) / u)}


def reference(hidden, head_words, head_scales, base, omega, pinv):
    w = unpack4(head_words, head_scales)
    logits = mxq(f64(hidden), 1, "e4m3") @ w
    y = (logits - f64(base)) * f64(omega)[:, None]
    phi = mxq(f64(pinv), 1, "e4m3") @ mxq(y, 0, "e5m2")
    return phi

@@ -1,0 +1,273 @@
+from contextlib import ExitStack
+
+import concourse.mybir as mybir
+from concourse.masks import make_identity
+
+S, K, C, F = 2048, 1536, 1024, 512
+FLOPS = 2 * S * K * C + 2 * F * S * C
+
+F32 = mybir.dt.float32
+BF16 = mybir.dt.bfloat16
+I32 = mybir.dt.int32
+U32 = mybir.dt.uint32
+U8 = mybir.dt.uint8
+E4M3 = mybir.dt.float8_e4m3fn_x4
+E5M2 = mybir.dt.float8_e5m2_x4
+E2M1 = mybir.dt.float4_e2m1fn_x4
+ALU = mybir.AluOpType
+ACT = mybir.ActivationFunctionType
+
+P = 128
+PACK = 4
+PASS = P * PACK
+N = 512
+K_PASSES = K // PASS
+S_PASSES = S // PASS
+STEPS = 2 * S_PASSES
+HALVES = C // N
+F_TILES = F // P
+PINV_UNITS = 2 * F_TILES
+
+
+def tile_kernel_shap_logits_s9_kernel(tc, hidden, head_words, head_scales, base, omega, pinv, out):
+    nc = tc.nc
+    with ExitStack() as ctx:
+        keep = ctx.enter_context(tc.tile_pool(name="keep", bufs=1))
+        work = ctx.enter_context(tc.tile_pool(name="work", bufs=4))
+        psum = ctx.enter_context(tc.psum_pool(name="psum", bufs=4))
+        ctx.enter_context(tc.manual_schedule())
+
+        w_scale = keep.tile([P, K_PASSES, C], U8, name="w_scale", align_bytes=64)
+        nc.vector.memset(w_scale[:].rearrange("p g n -> p (g n)").bitcast(I32), 0)
+        ident = keep.tile([P, P], F32, name="ident")
+        make_identity(nc, ident[:])
+
+        raw = {}
+        hidden_rows = hidden.rearrange("(g p h e) (q k) -> g h q p e k", p=P, h=2, e=2, k=PASS)
+        pinv_rows = pinv.rearrange("(j p) (a e k) -> j a p e k", p=P, e=2, k=PASS)
+
+        def load_unit(key, rows):
+            t = keep.tile([P, 2, PASS], BF16, name="raw_%s_%d_%d" % key)
+            nc.sync.dma_start(out=t[:], in_=rows)
+            raw[key] = t
+
+        def load_hidden(i):
+            for q in range(K_PASSES):
+                load_unit(("h", i, q), hidden_rows[i // 2, i % 2, q])
+
+        def load_pinv(n):
+            load_unit(("p", n // 2, n % 2), pinv_rows[n // 2, n % 2])
+
+        w_codes = []
+
+        def load_w(ch):
+            t = keep.tile([P, K_PASSES, 2 * N], U8, name="w_codes_%d" % ch, align_bytes=64)
+            src = head_words[:, :, 2 * N * ch : 2 * N * (ch + 1)].rearrange("g p n -> p g n")
+            nc.sync.dma_start(out=t[:].bitcast(I32), in_=src.bitcast(I32))
+            w_codes.append(t)
+
+        load_hidden(0)
+        load_w(0)
+        for r in range(4):
+            src = head_scales[:, r::4, :].rearrange("g q n -> q g n")
+            nc.sync.dma_start(out=w_scale[r:P:32, :, :].bitcast(I32), in_=src.bitcast(I32))
+        base_cols = keep.tile([P, C // P], BF16, name="base_cols")
+        nc.sync.dma_start(out=base_cols[:], in_=base.rearrange("(p m) -> p m", p=P))
+        omega_bf = keep.tile([P, S_PASSES, PACK], BF16, name="omega_bf")
+        nc.sync.dma_start(out=omega_bf[:], in_=omega.rearrange("(g p t) -> p g t", p=P, t=PACK))
+        load_hidden(1)
+        load_w(1)
+        for i in range(2, STEPS):
+            load_hidden(i)
+            load_pinv(i - 2)
+        load_pinv(PINV_UNITS - 2)
+        load_pinv(PINV_UNITS - 1)
+
+        grouped = {}
+        quantised = {}
+
+        def turn(key):
+            words = raw[key][:].rearrange("p e k -> p (e k)").bitcast(F32)
+            bank = psum.tile([P, 2, 2, P], F32, name="turn_bank", tag="turn")
+            for e in range(2):
+                for u in range(2):
+                    nc.tensor.transpose(bank[:, e, u, :], words[:, 2 * P * e + u : 2 * P * (e + 1) : 2], ident[:])
+            t = work.tile([P, 2 * PASS], BF16, name="grouped", bufs=8, align_bytes=64)
+            nc.scalar.copy(
+                out=t[:].bitcast(F32).rearrange("p (e m u) -> p e m u", e=2, u=2),
+                in_=bank[:].rearrange("p e u m -> p e m u"),
+            )
+            grouped[key] = t
+
+        def quantise(key):
+            codes = keep.tile([P, 2 * P], U32, name="codes_%s_%d_%d" % key, align_bytes=64)
+            scale = keep.tile([P, 2 * P], U8, name="scale_%s_%d_%d" % key, align_bytes=64)
+            nc.vector.quantize_mx(out=codes[:].bitcast(E4M3), scales=scale[:], in_=grouped[key][:])
+            quantised[key] = (codes, scale)
+
+        omega_f = keep.tile([P, S_PASSES * PACK], F32, name="omega_f")
+        base_rows = keep.tile([P, C], BF16, name="base_rows")
+
+        def spread_base():
+            words = base_cols[:].bitcast(F32)
+            bank = psum.tile([P, 4, P], F32, name="base_bank", tag="turn")
+            for w in range(4):
+                nc.tensor.transpose(bank[:, w, :], words[:, w : w + 1].to_broadcast([P, P]), ident[:])
+            nc.scalar.copy(
+                out=base_rows[:].bitcast(F32).rearrange("p (n w) -> p n w", w=4),
+                in_=bank[:].rearrange("p w n -> p n w"),
+            )
+
+        offsets = {}
+
+        def make_offsets(i):
+            for e in range(2):
+                slot = 2 * i + e
+                t = work.tile([P, C], F32, name="offset", bufs=6)
+                nc.scalar.activation(out=t[:], in_=base_rows[:], func=ACT.Copy, scale=omega_f[:, slot : slot + 1])
+                offsets[slot] = t
+
+        y_rows = {}
+        y_grouped = {}
+        y_quantised = {}
+        logits = {}
+
+        def logits_group(i, ch, e):
+            bank = psum.tile([P, N], F32, name="logits_bank", tag="sum")
+            for q in range(K_PASSES):
+                codes, scale = quantised[("h", i, q)]
+                nc.tensor.matmul_mx(
+                    out=bank[:],
+                    lhsT=codes[:, P * e : P * (e + 1)].bitcast(E4M3),
+                    lhsT_scale=scale[:, P * e : P * (e + 1)],
+                    rhs=w_codes[ch][:, q, :].bitcast(E2M1),
+                    rhs_scale=w_scale[:, q, N * ch : N * (ch + 1)],
+                    start=(q == 0),
+                    stop=(q == K_PASSES - 1),
+                )
+            logits[(i, ch, e)] = bank
+
+        def respond(i, ch, e):
+            g, slot = i // 2, 2 * i + e
+            if (g, ch) not in y_rows:
+                y_rows[(g, ch)] = work.tile([P, PACK, N], BF16, name="y_rows")
+            nc.vector.scalar_tensor_tensor(
+                out=y_rows[(g, ch)][:, slot % PACK, :],
+                in0=logits[(i, ch, e)][:],
+                scalar=omega_f[:, slot : slot + 1],
+                in1=offsets[slot][:, N * ch : N * (ch + 1)],
+                op0=ALU.mult,
+                op1=ALU.subtract,
+            )
+
+        def interleave_y(g, ch):
+            t = work.tile([P, N * PACK], BF16, name="y_grouped", bufs=3, align_bytes=64)
+            nc.vector.tensor_copy(
+                out=t[:].rearrange("p (c i t) -> p c t i", i=4, t=PACK),
+                in_=y_rows[(g, ch)][:].rearrange("p t (c i) -> p c t i", i=4),
+            )
+            y_grouped[(g, ch)] = t
+
+        def quantise_y(g, ch):
+            codes = keep.tile([P, N], U32, name="y_codes_%d_%d" % (g, ch), align_bytes=64)
+            scale = keep.tile([P, N], U8, name="y_scale_%d_%d" % (g, ch), align_bytes=64)
+            nc.vector.quantize_mx(out=codes[:].bitcast(E5M2), scales=scale[:], in_=y_grouped[(g, ch)][:])
+            y_quantised[(g, ch)] = (codes, scale)
+
+        phi = {}
+
+        def phi_pass(j, ch, g):
+            if g == 0:
+                phi[(j, ch)] = psum.tile([P, N], F32, name="phi_bank", tag="turn" if ch == 0 else "sum")
+            p_codes, p_scale = quantised[("p", j, g // 2)]
+            y_codes, y_scale = y_quantised[(g, ch)]
+            cols = slice(P * (g % 2), P * (g % 2 + 1))
+            nc.tensor.matmul_mx(
+                out=phi[(j, ch)][:],
+                lhsT=p_codes[:, cols].bitcast(E4M3),
+                lhsT_scale=p_scale[:, cols],
+                rhs=y_codes[:].bitcast(E5M2),
+                rhs_scale=y_scale[:],
+                start=(g == 0),
+                stop=(g == S_PASSES - 1),
+            )
+
+        def store_phi(j, ch):
+            t = keep.tile([P, N], F32, name="phi_%d_%d" % (j, ch))
+            if j % 2 == 0:
+                nc.scalar.copy(out=t[:], in_=phi[(j, ch)][:])
+            else:
+                nc.vector.tensor_copy(out=t[:], in_=phi[(j, ch)][:])
+            nc.sync.dma_start(out=out[P * j : P * (j + 1), N * ch : N * (ch + 1)], in_=t[:])
+
+        def units_of(i):
+            if i == STEPS:
+                return [("p", F_TILES - 1, 0), ("p", F_TILES - 1, 1)]
+            keys = [("h", i, q) for q in range(K_PASSES)]
+            if i >= 2:
+                keys.append(("p", (i - 2) // 2, (i - 2) % 2))
+            return keys
+
+        for key in units_of(0):
+            turn(key)
+            quantise(key)
+        nc.vector.tensor_copy(out=omega_f[:], in_=omega_bf[:].rearrange("p g t -> p (g t)"))
+        spread_base()
+        make_offsets(0)
+        for e in range(2):
+            logits_group(0, 0, e)
+        for key in units_of(1):
+            turn(key)
+        make_offsets(1)
+        for e in range(2):
+            respond(0, 0, e)
+        for e in range(2):
+            logits_group(0, 1, e)
+            quantise(("h", 1, e))
+            respond(0, 1, e)
+        quantise(("h", 1, 2))
+
+        pending = []
+        for i in range(1, STEPS):
+            ahead = units_of(i + 1)
+            for key in ahead:
+                turn(key)
+            if i + 1 < STEPS:
+                make_offsets(i + 1)
+            quantise(ahead[0])
+            for half in pending:
+                quantise_y(*half)
+            quantise(ahead[1])
+            logits_group(i, 0, 0)
+            respond(i, 0, 0)
+            for key in ahead[2:]:
+                quantise(key)
+            logits_group(i, 0, 1)
+            respond(i, 0, 1)
+            if i == STEPS - 1:
+                break
+            for e in range(2):
+                logits_group(i, 1, e)
+                respond(i, 1, e)
+            pending = [((i - 1) // 2, (i - 1) % 2)]
+            interleave_y(*pending[0])
+
+        last, g_last = STEPS - 1, S_PASSES - 1
+        interleave_y(g_last, 0)
+        logits_group(last, 1, 0)
+        respond(last, 1, 0)
+        quantise_y(g_last, 0)
+        logits_group(last, 1, 1)
+        respond(last, 1, 1)
+        interleave_y(g_last, 1)
+        for j in range(F_TILES):
+            for g in range(g_last):
+                phi_pass(j, 0, g)
+        quantise_y(g_last, 1)
+        for j in range(F_TILES):
+            phi_pass(j, 0, g_last)
+            store_phi(j, 0)
+        for j in range(F_TILES):
+            for g in range(S_PASSES):
+                phi_pass(j, 1, g)
+            store_phi(j, 1)

@@ -83,27 +83,45 @@ def tile_kernel_shap_logits_s9_kernel(tc, hidden, head_words, head_scales, base,
         load_pinv(PINV_UNITS - 2)
         load_pinv(PINV_UNITS - 1)
 
+        by_parity = {}
         grouped = {}
         quantised = {}
 
-        def turn(key):
-            words = raw[key][:].rearrange("p e k -> p (e k)").bitcast(F32)
-            bank = psum.tile([P, 2, 2, P], F32, name="turn_bank", tag="turn")
-            for e in range(2):
-                for u in range(2):
-                    nc.tensor.transpose(bank[:, e, u, :], words[:, 2 * P * e + u : 2 * P * (e + 1) : 2], ident[:])
-            t = work.tile([P, 2 * PASS], BF16, name="grouped", bufs=8, align_bytes=64)
-            nc.scalar.copy(
-                out=t[:].bitcast(F32).rearrange("p (e m u) -> p e m u", e=2, u=2),
-                in_=bank[:].rearrange("p e u m -> p e m u"),
-            )
-            grouped[key] = t
+        def words_of(key):
+            return raw[key][:].rearrange("p e k -> p (e k)").bitcast(F32)
 
-        def quantise(key):
-            codes = keep.tile([P, 2 * P], U32, name="codes_%s_%d_%d" % key, align_bytes=64)
-            scale = keep.tile([P, 2 * P], U8, name="scale_%s_%d_%d" % key, align_bytes=64)
-            nc.vector.quantize_mx(out=codes[:].bitcast(E4M3), scales=scale[:], in_=grouped[key][:])
-            quantised[key] = (codes, scale)
+        def sort_words(key):
+            t = work.tile([P, PASS], F32, name="by_parity", bufs=2)
+            nc.scalar.copy(
+                out=t[:].rearrange("p (u n i) -> p n u i", u=2, i=4),
+                in_=words_of(key).rearrange("p (n i u) -> p n u i", u=2, i=4),
+            )
+            by_parity[key] = t
+
+        def turn(keys):
+            t = work.tile([P, len(keys) * 2 * PASS], BF16, name="grouped", bufs=3, align_bytes=64)
+            for n, key in enumerate(keys):
+                bank = psum.tile([P, 2, 2, P], F32, name="turn_bank", tag="turn")
+                for e in range(2):
+                    for u in range(2):
+                        if key in by_parity:
+                            src = by_parity[key][:, 2 * P * u + P * e : 2 * P * u + P * (e + 1)]
+                        else:
+                            src = words_of(key)[:, 2 * P * e + u : 2 * P * (e + 1) : 2]
+                        nc.tensor.transpose(bank[:, e, u, :], src, ident[:])
+                nc.scalar.copy(
+                    out=t[:].bitcast(F32)[:, PASS * n : PASS * (n + 1)].rearrange("p (e m u) -> p e m u", e=2, u=2),
+                    in_=bank[:].rearrange("p e u m -> p e m u"),
+                )
+            grouped[keys[0]] = t
+
+        def quantise(keys):
+            codes = keep.tile([P, len(keys) * 2 * P], U32, name="codes_%s_%d_%d" % keys[0], align_bytes=64)
+            scale = keep.tile([P, len(keys) * 2 * P], U8, name="scale_%s_%d_%d" % keys[0], align_bytes=64)
+            nc.vector.quantize_mx(out=codes[:].bitcast(E4M3), scales=scale[:], in_=grouped[keys[0]][:])
+            for n, key in enumerate(keys):
+                cols = slice(2 * P * n, 2 * P * (n + 1))
+                quantised[key] = (codes[:, cols], scale[:, cols])
 
         omega_f = keep.tile([P, S_PASSES * PACK], F32, name="omega_f")
         base_rows = keep.tile([P, C], BF16, name="base_rows")
@@ -123,7 +141,7 @@ def tile_kernel_shap_logits_s9_kernel(tc, hidden, head_words, head_scales, base,
         def make_offsets(i):
             for e in range(2):
                 slot = 2 * i + e
-                t = work.tile([P, C], F32, name="offset", bufs=6)
+                t = work.tile([P, C], F32, name="offset", bufs=4)
                 nc.scalar.activation(out=t[:], in_=base_rows[:], func=ACT.Copy, scale=omega_f[:, slot : slot + 1])
                 offsets[slot] = t
 
@@ -132,25 +150,28 @@ def tile_kernel_shap_logits_s9_kernel(tc, hidden, head_words, head_scales, base,
         y_quantised = {}
         logits = {}
 
+        def logits_pass(i, ch, e, q):
+            if q == 0:
+                logits[(i, ch, e)] = psum.tile([P, N], F32, name="logits_bank", tag="sum")
+            codes, scale = quantised[("h", i, q)]
+            nc.tensor.matmul_mx(
+                out=logits[(i, ch, e)][:],
+                lhsT=codes[:, P * e : P * (e + 1)].bitcast(E4M3),
+                lhsT_scale=scale[:, P * e : P * (e + 1)],
+                rhs=w_codes[ch][:, q, :].bitcast(E2M1),
+                rhs_scale=w_scale[:, q, N * ch : N * (ch + 1)],
+                start=(q == 0),
+                stop=(q == K_PASSES - 1),
+            )
+
         def logits_group(i, ch, e):
-            bank = psum.tile([P, N], F32, name="logits_bank", tag="sum")
             for q in range(K_PASSES):
-                codes, scale = quantised[("h", i, q)]
-                nc.tensor.matmul_mx(
-                    out=bank[:],
-                    lhsT=codes[:, P * e : P * (e + 1)].bitcast(E4M3),
-                    lhsT_scale=scale[:, P * e : P * (e + 1)],
-                    rhs=w_codes[ch][:, q, :].bitcast(E2M1),
-                    rhs_scale=w_scale[:, q, N * ch : N * (ch + 1)],
-                    start=(q == 0),
-                    stop=(q == K_PASSES - 1),
-                )
-            logits[(i, ch, e)] = bank
+                logits_pass(i, ch, e, q)
 
         def respond(i, ch, e):
             g, slot = i // 2, 2 * i + e
             if (g, ch) not in y_rows:
-                y_rows[(g, ch)] = work.tile([P, PACK, N], BF16, name="y_rows")
+                y_rows[(g, ch)] = work.tile([P, PACK, N], BF16, name="y_rows_%d" % ch, bufs=2 + 2 * ch)
             nc.vector.scalar_tensor_tensor(
                 out=y_rows[(g, ch)][:, slot % PACK, :],
                 in0=logits[(i, ch, e)][:],
@@ -160,9 +181,9 @@ def tile_kernel_shap_logits_s9_kernel(tc, hidden, head_words, head_scales, base,
                 op1=ALU.subtract,
             )
 
-        def interleave_y(g, ch):
-            t = work.tile([P, N * PACK], BF16, name="y_grouped", bufs=3, align_bytes=64)
-            nc.vector.tensor_copy(
+        def interleave_y(g, ch, copy):
+            t = work.tile([P, N * PACK], BF16, name="y_grouped", bufs=4, align_bytes=64)
+            copy(
                 out=t[:].rearrange("p (c i t) -> p c t i", i=4, t=PACK),
                 in_=y_rows[(g, ch)][:].rearrange("p t (c i) -> p c t i", i=4),
             )
@@ -193,8 +214,8 @@ def tile_kernel_shap_logits_s9_kernel(tc, hidden, head_words, head_scales, base,
             )
 
         def store_phi(j, ch):
-            t = keep.tile([P, N], F32, name="phi_%d_%d" % (j, ch))
-            if j % 2 == 0:
+            t = work.tile([P, N], F32, name="phi_out")
+            if ch == 0 or j % 2 == 1:
                 nc.scalar.copy(out=t[:], in_=phi[(j, ch)][:])
             else:
                 nc.vector.tensor_copy(out=t[:], in_=phi[(j, ch)][:])
@@ -209,65 +230,73 @@ def tile_kernel_shap_logits_s9_kernel(tc, hidden, head_words, head_scales, base,
             return keys
 
         for key in units_of(0):
-            turn(key)
-            quantise(key)
+            turn([key])
+            quantise([key])
         nc.vector.tensor_copy(out=omega_f[:], in_=omega_bf[:].rearrange("p g t -> p (g t)"))
         spread_base()
         make_offsets(0)
-        for e in range(2):
-            logits_group(0, 0, e)
-        for key in units_of(1):
-            turn(key)
+        for q in range(K_PASSES):
+            for e in range(2):
+                logits_pass(0, 0, e, q)
+        turn(units_of(1)[:2])
+        turn(units_of(1)[2:])
         make_offsets(1)
         for e in range(2):
             respond(0, 0, e)
+        quantise(units_of(1)[:2])
+        quantise(units_of(1)[2:])
         for e in range(2):
             logits_group(0, 1, e)
-            quantise(("h", 1, e))
             respond(0, 1, e)
-        quantise(("h", 1, 2))
-
-        pending = []
-        for i in range(1, STEPS):
-            ahead = units_of(i + 1)
-            for key in ahead:
-                turn(key)
-            if i + 1 < STEPS:
-                make_offsets(i + 1)
-            quantise(ahead[0])
-            for half in pending:
-                quantise_y(*half)
-            quantise(ahead[1])
-            logits_group(i, 0, 0)
-            respond(i, 0, 0)
-            for key in ahead[2:]:
-                quantise(key)
-            logits_group(i, 0, 1)
-            respond(i, 0, 1)
-            if i == STEPS - 1:
-                break
-            for e in range(2):
-                logits_group(i, 1, e)
-                respond(i, 1, e)
-            pending = [((i - 1) // 2, (i - 1) % 2)]
-            interleave_y(*pending[0])
 
         last, g_last = STEPS - 1, S_PASSES - 1
-        interleave_y(g_last, 0)
+        pending = []
+        for i in range(1, last):
+            turn(units_of(i + 1))
+            sort_words(units_of(i + 2)[-1])
+            make_offsets(i + 1)
+            for ch in range(HALVES):
+                for e in range(2):
+                    logits_group(i, ch, e)
+                    respond(i, ch, e)
+                    if (ch, e) == (0, 0):
+                        quantise(units_of(i + 1))
+            for half in pending:
+                quantise_y(*half)
+            pending = [(i // 2, 0)] if i % 2 == 1 else [(0, 1)] if i == 2 else []
+            for half in pending:
+                interleave_y(*half, nc.vector.tensor_copy)
+
+        turn(units_of(STEPS))
+        for g in range(1, g_last):
+            interleave_y(g, 1, nc.scalar.copy)
+        logits_group(last, 0, 0)
+        respond(last, 0, 0)
+        quantise(units_of(STEPS))
+        logits_group(last, 0, 1)
+        respond(last, 0, 1)
+        interleave_y(g_last, 0, nc.vector.tensor_copy)
         logits_group(last, 1, 0)
         respond(last, 1, 0)
         quantise_y(g_last, 0)
         logits_group(last, 1, 1)
         respond(last, 1, 1)
-        interleave_y(g_last, 1)
+        interleave_y(g_last, 1, nc.vector.tensor_copy)
+        for g in range(1, S_PASSES):
+            quantise_y(g, 1)
         for j in range(F_TILES):
             for g in range(g_last):
                 phi_pass(j, 0, g)
-        quantise_y(g_last, 1)
         for j in range(F_TILES):
             phi_pass(j, 0, g_last)
             store_phi(j, 0)
-        for j in range(F_TILES):
+        for j in range(2):
+            for g in range(g_last):
+                phi_pass(j, 1, g)
+        for j in range(2):
+            phi_pass(j, 1, g_last)
+            store_phi(j, 1)
+        for j in range(2, F_TILES):
             for g in range(S_PASSES):
                 phi_pass(j, 1, g)
             store_phi(j, 1)

@@ -27,6 +27,8 @@ STEPS = 2 * S_PASSES
 HALVES = C // N
 F_TILES = F // P
 PINV_UNITS = 2 * F_TILES
+OFFSETS_AHEAD = 3
+GPSIMD_COLS = 768
 
 
 def tile_kernel_shap_logits_s9_kernel(tc, hidden, head_words, head_scales, base, omega, pinv, out):
@@ -78,8 +80,8 @@ def tile_kernel_shap_logits_s9_kernel(tc, hidden, head_words, head_scales, base,
         load_hidden(1)
         load_w(1)
         for i in range(2, STEPS):
-            load_hidden(i)
             load_pinv(i - 2)
+            load_hidden(i)
         load_pinv(PINV_UNITS - 2)
         load_pinv(PINV_UNITS - 1)
 
@@ -91,7 +93,7 @@ def tile_kernel_shap_logits_s9_kernel(tc, hidden, head_words, head_scales, base,
             return raw[key][:].rearrange("p e k -> p (e k)").bitcast(F32)
 
         def sort_words(key):
-            t = work.tile([P, PASS], F32, name="by_parity", bufs=2)
+            t = work.tile([P, PASS], F32, name="by_parity", bufs=3)
             nc.scalar.copy(
                 out=t[:].rearrange("p (u n i) -> p n u i", u=2, i=4),
                 in_=words_of(key).rearrange("p (n i u) -> p n u i", u=2, i=4),
@@ -138,12 +140,26 @@ def tile_kernel_shap_logits_s9_kernel(tc, hidden, head_words, head_scales, base,
 
         offsets = {}
 
-        def make_offsets(i):
-            for e in range(2):
-                slot = 2 * i + e
-                t = work.tile([P, C], F32, name="offset", bufs=4)
-                nc.scalar.activation(out=t[:], in_=base_rows[:], func=ACT.Copy, scale=omega_f[:, slot : slot + 1])
-                offsets[slot] = t
+        def begin_offset(slot):
+            if slot < 2 * STEPS:
+                offsets[slot] = work.tile([P, C], F32, name="offset", bufs=OFFSETS_AHEAD)
+                nc.gpsimd.tensor_scalar(
+                    out=offsets[slot][:, :GPSIMD_COLS],
+                    in0=base_rows[:, :GPSIMD_COLS],
+                    scalar1=omega_f[:, slot : slot + 1],
+                    scalar2=0.0,
+                    op0=ALU.mult,
+                    op1=ALU.add,
+                )
+
+        def finish_offset(slot):
+            if slot < 2 * STEPS:
+                nc.scalar.activation(
+                    out=offsets[slot][:, GPSIMD_COLS:],
+                    in_=base_rows[:, GPSIMD_COLS:],
+                    func=ACT.Copy,
+                    scale=omega_f[:, slot : slot + 1],
+                )
 
         y_rows = {}
         y_grouped = {}
@@ -224,23 +240,25 @@ def tile_kernel_shap_logits_s9_kernel(tc, hidden, head_words, head_scales, base,
         def units_of(i):
             if i == STEPS:
                 return [("p", F_TILES - 1, 0), ("p", F_TILES - 1, 1)]
-            keys = [("h", i, q) for q in range(K_PASSES)]
-            if i >= 2:
-                keys.append(("p", (i - 2) // 2, (i - 2) % 2))
-            return keys
+            keys = [("p", (i - 2) // 2, (i - 2) % 2)] if i >= 2 else []
+            return keys + [("h", i, q) for q in range(K_PASSES)]
 
         for key in units_of(0):
             turn([key])
             quantise([key])
         nc.vector.tensor_copy(out=omega_f[:], in_=omega_bf[:].rearrange("p g t -> p (g t)"))
         spread_base()
-        make_offsets(0)
+        for slot in range(OFFSETS_AHEAD):
+            begin_offset(slot)
+        for key in units_of(1):
+            sort_words(key)
         for q in range(K_PASSES):
             for e in range(2):
                 logits_pass(0, 0, e, q)
         turn(units_of(1)[:2])
         turn(units_of(1)[2:])
-        make_offsets(1)
+        for slot in range(OFFSETS_AHEAD):
+            finish_offset(slot)
         for e in range(2):
             respond(0, 0, e)
         quantise(units_of(1)[:2])
@@ -248,26 +266,33 @@ def tile_kernel_shap_logits_s9_kernel(tc, hidden, head_words, head_scales, base,
         for e in range(2):
             logits_group(0, 1, e)
             respond(0, 1, e)
+            begin_offset(e + OFFSETS_AHEAD)
 
         last, g_last = STEPS - 1, S_PASSES - 1
-        pending = []
         for i in range(1, last):
             turn(units_of(i + 1))
-            sort_words(units_of(i + 2)[-1])
-            make_offsets(i + 1)
-            for ch in range(HALVES):
-                for e in range(2):
+            finish_offset(2 * i + 1)
+            finish_offset(2 * i + 2)
+            if i + 2 < STEPS:
+                for key in units_of(i + 2)[1:]:
+                    sort_words(key)
+            else:
+                interleave_y(0, 1, nc.scalar.copy)
+            for e in range(2):
+                for ch in range(HALVES):
                     logits_group(i, ch, e)
                     respond(i, ch, e)
-                    if (ch, e) == (0, 0):
-                        quantise(units_of(i + 1))
-            for half in pending:
-                quantise_y(*half)
-            pending = [(i // 2, 0)] if i % 2 == 1 else [(0, 1)] if i == 2 else []
-            for half in pending:
-                interleave_y(*half, nc.vector.tensor_copy)
+                begin_offset(2 * i + e + OFFSETS_AHEAD)
+                if e == 0:
+                    quantise(units_of(i + 1))
+            if i % 2 == 1:
+                interleave_y(i // 2, 0, nc.vector.tensor_copy)
+            else:
+                quantise_y(i // 2 - 1, 0)
 
         turn(units_of(STEPS))
+        finish_offset(2 * last + 1)
+        quantise_y(0, 1)
         for g in range(1, g_last):
             interleave_y(g, 1, nc.scalar.copy)
         logits_group(last, 0, 0)

@@ -92,9 +92,9 @@ def tile_kernel_shap_logits_s9_kernel(tc, hidden, head_words, head_scales, base,
         def words_of(key):
             return raw[key][:].rearrange("p e k -> p (e k)").bitcast(F32)
 
-        def sort_words(key):
-            t = work.tile([P, PASS], F32, name="by_parity", bufs=3)
-            nc.scalar.copy(
+        def sort_words(key, copy):
+            t = work.tile([P, PASS], F32, name="by_parity")
+            copy(
                 out=t[:].rearrange("p (u n i) -> p n u i", u=2, i=4),
                 in_=words_of(key).rearrange("p (n i u) -> p n u i", u=2, i=4),
             )
@@ -229,13 +229,14 @@ def tile_kernel_shap_logits_s9_kernel(tc, hidden, head_words, head_scales, base,
                 stop=(g == S_PASSES - 1),
             )
 
-        def store_phi(j, ch):
+        def store_phi(j, ch, pieces):
+            copy = nc.scalar.copy if ch == 0 or j % 2 == 1 else nc.vector.tensor_copy
             t = work.tile([P, N], F32, name="phi_out")
-            if ch == 0 or j % 2 == 1:
-                nc.scalar.copy(out=t[:], in_=phi[(j, ch)][:])
-            else:
-                nc.vector.tensor_copy(out=t[:], in_=phi[(j, ch)][:])
-            nc.sync.dma_start(out=out[P * j : P * (j + 1), N * ch : N * (ch + 1)], in_=t[:])
+            width = N // pieces
+            for c0 in range(0, N, width):
+                copy(out=t[:, c0 : c0 + width], in_=phi[(j, ch)][:, c0 : c0 + width])
+                dst = out[P * j : P * (j + 1), N * ch + c0 : N * ch + c0 + width]
+                nc.sync.dma_start(out=dst, in_=t[:, c0 : c0 + width])
 
         def units_of(i):
             if i == STEPS:
@@ -244,6 +245,8 @@ def tile_kernel_shap_logits_s9_kernel(tc, hidden, head_words, head_scales, base,
             return keys + [("h", i, q) for q in range(K_PASSES)]
 
         for key in units_of(0):
+            sort_words(key, nc.vector.tensor_copy)
+        for key in units_of(0):
             turn([key])
             quantise([key])
         nc.vector.tensor_copy(out=omega_f[:], in_=omega_bf[:].rearrange("p g t -> p (g t)"))
@@ -251,7 +254,7 @@ def tile_kernel_shap_logits_s9_kernel(tc, hidden, head_words, head_scales, base,
         for slot in range(OFFSETS_AHEAD):
             begin_offset(slot)
         for key in units_of(1):
-            sort_words(key)
+            sort_words(key, nc.scalar.copy)
         for q in range(K_PASSES):
             for e in range(2):
                 logits_pass(0, 0, e, q)
@@ -261,6 +264,8 @@ def tile_kernel_shap_logits_s9_kernel(tc, hidden, head_words, head_scales, base,
             finish_offset(slot)
         for e in range(2):
             respond(0, 0, e)
+        for key in units_of(2):
+            sort_words(key, nc.vector.tensor_copy)
         quantise(units_of(1)[:2])
         quantise(units_of(1)[2:])
         for e in range(2):
@@ -275,7 +280,7 @@ def tile_kernel_shap_logits_s9_kernel(tc, hidden, head_words, head_scales, base,
             finish_offset(2 * i + 2)
             if i + 2 < STEPS:
                 for key in units_of(i + 2)[1:]:
-                    sort_words(key)
+                    sort_words(key, nc.scalar.copy)
             else:
                 interleave_y(0, 1, nc.scalar.copy)
             for e in range(2):
@@ -314,14 +319,13 @@ def tile_kernel_shap_logits_s9_kernel(tc, hidden, head_words, head_scales, base,
                 phi_pass(j, 0, g)
         for j in range(F_TILES):
             phi_pass(j, 0, g_last)
-            store_phi(j, 0)
-        for j in range(2):
-            for g in range(g_last):
+            store_phi(j, 0, 1)
+        for g in range(g_last):
+            for j in range(F_TILES - 1):
                 phi_pass(j, 1, g)
-        for j in range(2):
+        for j in range(F_TILES - 1):
             phi_pass(j, 1, g_last)
-            store_phi(j, 1)
-        for j in range(2, F_TILES):
-            for g in range(S_PASSES):
-                phi_pass(j, 1, g)
-            store_phi(j, 1)
+            store_phi(j, 1, 1)
+        for g in range(S_PASSES):
+            phi_pass(F_TILES - 1, 1, g)
+        store_phi(F_TILES - 1, 1, 2)

from contextlib import ExitStack

import concourse.mybir as mybir
from concourse.masks import make_identity

S, K, C, F = 2048, 1536, 1024, 512
FLOPS = 2 * S * K * C + 2 * F * S * C

F32 = mybir.dt.float32
BF16 = mybir.dt.bfloat16
I32 = mybir.dt.int32
U32 = mybir.dt.uint32
U8 = mybir.dt.uint8
E4M3 = mybir.dt.float8_e4m3fn_x4
E5M2 = mybir.dt.float8_e5m2_x4
E2M1 = mybir.dt.float4_e2m1fn_x4
ALU = mybir.AluOpType
ACT = mybir.ActivationFunctionType

P = 128
PACK = 4
PASS = P * PACK
N = 512
K_PASSES = K // PASS
S_PASSES = S // PASS
STEPS = 2 * S_PASSES
HALVES = C // N
F_TILES = F // P
PINV_UNITS = 2 * F_TILES
OFFSETS_AHEAD = 3
GPSIMD_COLS = 768


def tile_kernel_shap_logits_s9_kernel(tc, hidden, head_words, head_scales, base, omega, pinv, out):
    nc = tc.nc
    with ExitStack() as ctx:
        keep = ctx.enter_context(tc.tile_pool(name="keep", bufs=1))
        work = ctx.enter_context(tc.tile_pool(name="work", bufs=4))
        psum = ctx.enter_context(tc.psum_pool(name="psum", bufs=4))
        ctx.enter_context(tc.manual_schedule())

        w_scale = keep.tile([P, K_PASSES, C], U8, name="w_scale", align_bytes=64)
        nc.vector.memset(w_scale[:].rearrange("p g n -> p (g n)").bitcast(I32), 0)
        ident = keep.tile([P, P], F32, name="ident")
        make_identity(nc, ident[:])

        raw = {}
        hidden_rows = hidden.rearrange("(g p h e) (q k) -> g h q p e k", p=P, h=2, e=2, k=PASS)
        pinv_rows = pinv.rearrange("(j p) (a e k) -> j a p e k", p=P, e=2, k=PASS)

        def load_unit(key, rows):
            t = keep.tile([P, 2, PASS], BF16, name="raw_%s_%d_%d" % key)
            nc.sync.dma_start(out=t[:], in_=rows)
            raw[key] = t

        def load_hidden(i):
            for q in range(K_PASSES):
                load_unit(("h", i, q), hidden_rows[i // 2, i % 2, q])

        def load_pinv(n):
            load_unit(("p", n // 2, n % 2), pinv_rows[n // 2, n % 2])

        w_codes = []

        def load_w(ch):
            t = keep.tile([P, K_PASSES, 2 * N], U8, name="w_codes_%d" % ch, align_bytes=64)
            src = head_words[:, :, 2 * N * ch : 2 * N * (ch + 1)].rearrange("g p n -> p g n")
            nc.sync.dma_start(out=t[:].bitcast(I32), in_=src.bitcast(I32))
            w_codes.append(t)

        load_hidden(0)
        load_w(0)
        for r in range(4):
            src = head_scales[:, r::4, :].rearrange("g q n -> q g n")
            nc.sync.dma_start(out=w_scale[r:P:32, :, :].bitcast(I32), in_=src.bitcast(I32))
        base_cols = keep.tile([P, C // P], BF16, name="base_cols")
        nc.sync.dma_start(out=base_cols[:], in_=base.rearrange("(p m) -> p m", p=P))
        omega_bf = keep.tile([P, S_PASSES, PACK], BF16, name="omega_bf")
        nc.sync.dma_start(out=omega_bf[:], in_=omega.rearrange("(g p t) -> p g t", p=P, t=PACK))
        load_hidden(1)
        load_w(1)
        for i in range(2, STEPS):
            load_pinv(i - 2)
            load_hidden(i)
        load_pinv(PINV_UNITS - 2)
        load_pinv(PINV_UNITS - 1)

        by_parity = {}
        grouped = {}
        quantised = {}

        def words_of(key):
            return raw[key][:].rearrange("p e k -> p (e k)").bitcast(F32)

        def sort_words(key, copy):
            t = work.tile([P, PASS], F32, name="by_parity")
            copy(
                out=t[:].rearrange("p (u n i) -> p n u i", u=2, i=4),
                in_=words_of(key).rearrange("p (n i u) -> p n u i", u=2, i=4),
            )
            by_parity[key] = t

        def turn(keys):
            t = work.tile([P, len(keys) * 2 * PASS], BF16, name="grouped", bufs=3, align_bytes=64)
            for n, key in enumerate(keys):
                bank = psum.tile([P, 2, 2, P], F32, name="turn_bank", tag="turn")
                for e in range(2):
                    for u in range(2):
                        if key in by_parity:
                            src = by_parity[key][:, 2 * P * u + P * e : 2 * P * u + P * (e + 1)]
                        else:
                            src = words_of(key)[:, 2 * P * e + u : 2 * P * (e + 1) : 2]
                        nc.tensor.transpose(bank[:, e, u, :], src, ident[:])
                nc.scalar.copy(
                    out=t[:].bitcast(F32)[:, PASS * n : PASS * (n + 1)].rearrange("p (e m u) -> p e m u", e=2, u=2),
                    in_=bank[:].rearrange("p e u m -> p e m u"),
                )
            grouped[keys[0]] = t

        def quantise(keys):
            codes = keep.tile([P, len(keys) * 2 * P], U32, name="codes_%s_%d_%d" % keys[0], align_bytes=64)
            scale = keep.tile([P, len(keys) * 2 * P], U8, name="scale_%s_%d_%d" % keys[0], align_bytes=64)
            nc.vector.quantize_mx(out=codes[:].bitcast(E4M3), scales=scale[:], in_=grouped[keys[0]][:])
            for n, key in enumerate(keys):
                cols = slice(2 * P * n, 2 * P * (n + 1))
                quantised[key] = (codes[:, cols], scale[:, cols])

        omega_f = keep.tile([P, S_PASSES * PACK], F32, name="omega_f")
        base_rows = keep.tile([P, C], BF16, name="base_rows")

        def spread_base():
            words = base_cols[:].bitcast(F32)
            bank = psum.tile([P, 4, P], F32, name="base_bank", tag="turn")
            for w in range(4):
                nc.tensor.transpose(bank[:, w, :], words[:, w : w + 1].to_broadcast([P, P]), ident[:])
            nc.scalar.copy(
                out=base_rows[:].bitcast(F32).rearrange("p (n w) -> p n w", w=4),
                in_=bank[:].rearrange("p w n -> p n w"),
            )

        offsets = {}

        def begin_offset(slot):
            if slot < 2 * STEPS:
                offsets[slot] = work.tile([P, C], F32, name="offset", bufs=OFFSETS_AHEAD)
                nc.gpsimd.tensor_scalar(
                    out=offsets[slot][:, :GPSIMD_COLS],
                    in0=base_rows[:, :GPSIMD_COLS],
                    scalar1=omega_f[:, slot : slot + 1],
                    scalar2=0.0,
                    op0=ALU.mult,
                    op1=ALU.add,
                )

        def finish_offset(slot):
            if slot < 2 * STEPS:
                nc.scalar.activation(
                    out=offsets[slot][:, GPSIMD_COLS:],
                    in_=base_rows[:, GPSIMD_COLS:],
                    func=ACT.Copy,
                    scale=omega_f[:, slot : slot + 1],
                )

        y_rows = {}
        y_grouped = {}
        y_quantised = {}
        logits = {}

        def logits_pass(i, ch, e, q):
            if q == 0:
                logits[(i, ch, e)] = psum.tile([P, N], F32, name="logits_bank", tag="sum")
            codes, scale = quantised[("h", i, q)]
            nc.tensor.matmul_mx(
                out=logits[(i, ch, e)][:],
                lhsT=codes[:, P * e : P * (e + 1)].bitcast(E4M3),
                lhsT_scale=scale[:, P * e : P * (e + 1)],
                rhs=w_codes[ch][:, q, :].bitcast(E2M1),
                rhs_scale=w_scale[:, q, N * ch : N * (ch + 1)],
                start=(q == 0),
                stop=(q == K_PASSES - 1),
            )

        def logits_group(i, ch, e):
            for q in range(K_PASSES):
                logits_pass(i, ch, e, q)

        def respond(i, ch, e):
            g, slot = i // 2, 2 * i + e
            if (g, ch) not in y_rows:
                y_rows[(g, ch)] = work.tile([P, PACK, N], BF16, name="y_rows_%d" % ch, bufs=2 + 2 * ch)
            nc.vector.scalar_tensor_tensor(
                out=y_rows[(g, ch)][:, slot % PACK, :],
                in0=logits[(i, ch, e)][:],
                scalar=omega_f[:, slot : slot + 1],
                in1=offsets[slot][:, N * ch : N * (ch + 1)],
                op0=ALU.mult,
                op1=ALU.subtract,
            )

        def interleave_y(g, ch, copy):
            t = work.tile([P, N * PACK], BF16, name="y_grouped", bufs=4, align_bytes=64)
            copy(
                out=t[:].rearrange("p (c i t) -> p c t i", i=4, t=PACK),
                in_=y_rows[(g, ch)][:].rearrange("p t (c i) -> p c t i", i=4),
            )
            y_grouped[(g, ch)] = t

        def quantise_y(g, ch):
            codes = keep.tile([P, N], U32, name="y_codes_%d_%d" % (g, ch), align_bytes=64)
            scale = keep.tile([P, N], U8, name="y_scale_%d_%d" % (g, ch), align_bytes=64)
            nc.vector.quantize_mx(out=codes[:].bitcast(E5M2), scales=scale[:], in_=y_grouped[(g, ch)][:])
            y_quantised[(g, ch)] = (codes, scale)

        phi = {}

        def phi_pass(j, ch, g):
            if g == 0:
                phi[(j, ch)] = psum.tile([P, N], F32, name="phi_bank", tag="turn" if ch == 0 else "sum")
            p_codes, p_scale = quantised[("p", j, g // 2)]
            y_codes, y_scale = y_quantised[(g, ch)]
            cols = slice(P * (g % 2), P * (g % 2 + 1))
            nc.tensor.matmul_mx(
                out=phi[(j, ch)][:],
                lhsT=p_codes[:, cols].bitcast(E4M3),
                lhsT_scale=p_scale[:, cols],
                rhs=y_codes[:].bitcast(E5M2),
                rhs_scale=y_scale[:],
                start=(g == 0),
                stop=(g == S_PASSES - 1),
            )

        def store_phi(j, ch, pieces):
            copy = nc.scalar.copy if ch == 0 or j % 2 == 1 else nc.vector.tensor_copy
            t = work.tile([P, N], F32, name="phi_out")
            width = N // pieces
            for c0 in range(0, N, width):
                copy(out=t[:, c0 : c0 + width], in_=phi[(j, ch)][:, c0 : c0 + width])
                dst = out[P * j : P * (j + 1), N * ch + c0 : N * ch + c0 + width]
                nc.sync.dma_start(out=dst, in_=t[:, c0 : c0 + width])

        def units_of(i):
            if i == STEPS:
                return [("p", F_TILES - 1, 0), ("p", F_TILES - 1, 1)]
            keys = [("p", (i - 2) // 2, (i - 2) % 2)] if i >= 2 else []
            return keys + [("h", i, q) for q in range(K_PASSES)]

        for key in units_of(0):
            sort_words(key, nc.vector.tensor_copy)
        for key in units_of(0):
            turn([key])
            quantise([key])
        nc.vector.tensor_copy(out=omega_f[:], in_=omega_bf[:].rearrange("p g t -> p (g t)"))
        spread_base()
        for slot in range(OFFSETS_AHEAD):
            begin_offset(slot)
        for key in units_of(1):
            sort_words(key, nc.scalar.copy)
        for q in range(K_PASSES):
            for e in range(2):
                logits_pass(0, 0, e, q)
        turn(units_of(1)[:2])
        turn(units_of(1)[2:])
        for slot in range(OFFSETS_AHEAD):
            finish_offset(slot)
        for e in range(2):
            respond(0, 0, e)
        for key in units_of(2):
            sort_words(key, nc.vector.tensor_copy)
        quantise(units_of(1)[:2])
        quantise(units_of(1)[2:])
        for e in range(2):
            logits_group(0, 1, e)
            respond(0, 1, e)
            begin_offset(e + OFFSETS_AHEAD)

        last, g_last = STEPS - 1, S_PASSES - 1
        for i in range(1, last):
            turn(units_of(i + 1))
            finish_offset(2 * i + 1)
            finish_offset(2 * i + 2)
            if i + 2 < STEPS:
                for key in units_of(i + 2)[1:]:
                    sort_words(key, nc.scalar.copy)
            else:
                interleave_y(0, 1, nc.scalar.copy)
            for e in range(2):
                for ch in range(HALVES):
                    logits_group(i, ch, e)
                    respond(i, ch, e)
                begin_offset(2 * i + e + OFFSETS_AHEAD)
                if e == 0:
                    quantise(units_of(i + 1))
            if i % 2 == 1:
                interleave_y(i // 2, 0, nc.vector.tensor_copy)
            else:
                quantise_y(i // 2 - 1, 0)

        turn(units_of(STEPS))
        finish_offset(2 * last + 1)
        quantise_y(0, 1)
        for g in range(1, g_last):
            interleave_y(g, 1, nc.scalar.copy)
        logits_group(last, 0, 0)
        respond(last, 0, 0)
        quantise(units_of(STEPS))
        logits_group(last, 0, 1)
        respond(last, 0, 1)
        interleave_y(g_last, 0, nc.vector.tensor_copy)
        logits_group(last, 1, 0)
        respond(last, 1, 0)
        quantise_y(g_last, 0)
        logits_group(last, 1, 1)
        respond(last, 1, 1)
        interleave_y(g_last, 1, nc.vector.tensor_copy)
        for g in range(1, S_PASSES):
            quantise_y(g, 1)
        for j in range(F_TILES):
            for g in range(g_last):
                phi_pass(j, 0, g)
        for j in range(F_TILES):
            phi_pass(j, 0, g_last)
            store_phi(j, 0, 1)
        for g in range(g_last):
            for j in range(F_TILES - 1):
                phi_pass(j, 1, g)
        for j in range(F_TILES - 1):
            phi_pass(j, 1, g_last)
            store_phi(j, 1, 1)
        for g in range(S_PASSES):
            phi_pass(F_TILES - 1, 1, g)
        store_phi(F_TILES - 1, 1, 2)
